import numpy as np
import ml_dtypes


def mxq(x, axis, fmt="e4m3"):
    dtype, down = {"e4m3": (ml_dtypes.float8_e4m3fn, 7), "e5m2": (ml_dtypes.float8_e5m2, 14)}[fmt]
    v = np.moveaxis(np.asarray(x, np.float32).astype(ml_dtypes.bfloat16).astype(np.float64), axis, -1)
    blocks = v.reshape(v.shape[:-1] + (-1, 32))
    amax = np.abs(blocks).max(-1, keepdims=True)
    byte = np.maximum(np.where(amax > 0, np.frexp(amax)[1] - 1 + 127, 0) - down, 1)
    scale = np.exp2(byte - 127.0)
    codes = (blocks / scale).astype(np.float32).astype(dtype).astype(np.float64)
    return np.moveaxis((codes * scale).reshape(v.shape), -1, axis)


WIDE = False


def mx_kscale(k):
    if not WIDE:
        return np.ones(k)
    levels = np.array([30, -30])
    if k % 512:
        return np.exp2(np.random.permutation(np.resize(levels, k // 32))).repeat(32)
    a = np.empty((k // 512, 16))
    for p in range(k // 512):
        a[p, :8] = np.random.permutation(np.resize(levels, 8))
        for g in range(8):
            far = levels[np.abs(levels - a[p, g]) >= 10]
            a[p, g + 8] = far[np.random.randint(len(far))]
    return np.exp2(a.ravel()).repeat(32)


def f64(x):
    return np.asarray(x).astype(np.float64)


def striped(idx):
    return np.tile(np.asarray(idx).reshape(-1, 16).T, (8, 1)).astype(np.uint16)


def unstriped(offs):
    return offs[:16].T.reshape(-1).astype(np.int64)


E2M1 = np.array([0.0, 0.5, 1.0, 1.5, 2.0, 3.0, 4.0, 6.0, -0.0, -0.5, -1.0, -1.5, -2.0, -3.0, -4.0, -6.0])


def pack_weight(w, fmt):
    k, n = w.shape
    w = f64(np.asarray(w, np.float32).astype(ml_dtypes.bfloat16)).reshape(k // 32, 32, n)
    amax = np.abs(w).max(1)
    if fmt in ("e4m3", "e5m2"):
        byte = np.frexp(amax)[1] - 1 + 127 - (7 if fmt == "e4m3" else 14)
    else:
        mant, ex = np.frexp(amax / 6.0)
        byte = np.where(mant > 0.5, ex, ex - 1) + 127
    byte = np.clip(np.where(amax > 0, byte, 1), 1, 254)
    scaled = (w * np.exp2(127.0 - byte)[:, None, :]).reshape(k, n).astype(np.float32)
    by_word = np.ascontiguousarray(scaled.reshape(k // 512, 128, 4, n).transpose(0, 1, 3, 2))
    if fmt in ("e4m3", "e5m2"):
        words = by_word.astype(ml_dtypes.float8_e4m3fn if fmt == "e4m3" else ml_dtypes.float8_e5m2).view(np.uint8)
    else:
        c = by_word.astype(ml_dtypes.float4_e2m1fn).view(np.uint8) & 0xF
        words = (c[..., 0::2] | (c[..., 1::2] << 4)).reshape(k // 512, 128, 2 * n)
    return np.ascontiguousarray(words), np.ascontiguousarray(byte.astype(np.uint8).reshape(k // 512, 16, n))


def unpack_weight(words, scales, fmt):
    g, _, n = scales.shape
    words = np.ascontiguousarray(words).reshape(g, 128, n, -1)
    if fmt in ("e4m3", "e5m2"):
        vals = words.view(ml_dtypes.float8_e4m3fn if fmt == "e4m3" else ml_dtypes.float8_e5m2).astype(np.float64)
    else:
        nib = np.empty((g, 128, n, 4), np.uint8)
        nib[..., 0::2] = words & 0xF
        nib[..., 1::2] = words >> 4
        vals = E2M1[nib]
    vals = vals * np.repeat(np.exp2(scales.astype(np.float64) - 127.0), 8, axis=1)[..., None]
    return vals.transpose(0, 1, 3, 2).reshape(g * 512, n)


K, T, J, N, C = 1024, 1024, 256, 256, 1024


def setup_inputs():
    n = np.random.standard_normal
    idx = np.random.permutation(T)[:J]
    idx2 = np.random.permutation(C)[:N]
    fk = mx_kscale(K)
    xtp = pack_weight(n((K, T)) * np.random.uniform(0.4, 1.6, (1, T)) / fk[:, None], "e5m2")
    wap = pack_weight(n((K, N)) * 1 / np.sqrt(K) * fk[:, None], "e5m2")
    return {
        "xt_words": xtp[0],
        "xt_scales": xtp[1],
        "wa_words": wap[0],
        "wa_scales": wap[1],
        "wb": (n((K, N)) * 1 / np.sqrt(K) * fk[:, None]).astype(np.float32),
        "bi": (np.random.uniform(-0.6, 0.6, (1, N))).astype(np.float32),
        "old": (1.0 * n((J, C))).astype(np.float32),
        "offs": striped(idx),
        "offs2": striped(idx2),
    }


def reference(xt_words, xt_scales, wa_words, wa_scales, wb, bi, old, offs, offs2):
    idx = unstriped(offs)
    idx2 = unstriped(offs2)
    xtu = unpack_weight(xt_words, xt_scales, "e5m2")
    wau = unpack_weight(wa_words, wa_scales, "e5m2")
    xtidxg = xtu[:, idx]
    a = xtidxg.T @ wau
    wbq = mxq(f64(wb), 0, "e4m3")
    b0 = xtidxg.T @ wbq
    b2 = b0 + f64(bi)
    d = np.maximum(a, b2)
    pp = np.zeros((J, C))
    pp[:, idx2] = d
    y = pp - 0.4 * f64(old)
    return y

from contextlib import ExitStack

import concourse.mybir as mybir
from concourse.masks import make_identity

K, T, J, N, C = 1024, 1024, 256, 256, 1024
FLOPS = 2 * 2 * K * J * N

F32 = mybir.dt.float32
BF16 = mybir.dt.bfloat16
I32 = mybir.dt.int32
U32 = mybir.dt.uint32
U16 = mybir.dt.uint16
U8 = mybir.dt.uint8
E4M3X4 = mybir.dt.float8_e4m3fn_x4
E5M2X4 = mybir.dt.float8_e5m2_x4
ALU = mybir.AluOpType
COPY = mybir.ActivationFunctionType.Copy

P = 128
PACK = 4
PASSES = K // (P * PACK)
ROW_TILES = J // P
LIST_COLS = 16
STORE_COLS = 512


def tile_list_rows_onetoken_placedrows_kernel(
    tc, xt_words, xt_scales, wa_words, wa_scales, wb, bi, old, offs, offs2, out
):
    nc = tc.nc
    with ExitStack() as ctx:
        keep = ctx.enter_context(tc.tile_pool(name="keep", bufs=1))
        rows = ctx.enter_context(tc.tile_pool(name="rows", bufs=2))
        psum = ctx.enter_context(tc.psum_pool(name="psum", bufs=1))

        tokens = keep.tile([P, J // 16], U16, name="tokens")
        places = keep.tile([P, N // 16], U16, name="places")
        x_scales = keep.tile([P, PASSES, T], U8, name="x_scales", align_bytes=64)
        a_scales = keep.tile([P, PASSES, N], U8, name="a_scales", align_bytes=64)
        a_words = keep.tile([P, PASSES, N], I32, name="a_words", align_bytes=64)
        x_words = [keep.tile([P, T], I32, name=f"x_words{z}", align_bytes=64) for z in range(PASSES)]
        pages = [keep.tile([P, C], F32, name=f"page{r}") for r in range(ROW_TILES)]
        bias_cols = keep.tile([P, N // P], F32, name="bias_cols")
        ident = keep.tile([P, P], F32, name="ident")

        nc.vector.memset(x_scales[:].bitcast(I32), 0)
        nc.vector.memset(a_scales[:].bitcast(I32), 0)

        wb_raw = []
        for z in range(PASSES):
            raw = rows.tile([P, PACK, N], F32, name="rows")
            wb_raw.append(raw)

        def load_wb(z):
            nc.sync.dma_start(wb_raw[z][:], wb[z * P * PACK : (z + 1) * P * PACK, :].rearrange("(p j) n -> p j n", j=PACK))

        nc.sync.dma_start(tokens[:], offs)
        load_wb(0)
        nc.sync.dma_start(bias_cols[:], bi.rearrange("o (p c) -> p (o c)", p=P))
        nc.sync.dma_start(places[:], offs2)
        xs_rows = xt_scales.bitcast(I32).rearrange("z (q r) c -> r q z c", r=4)
        as_rows = wa_scales.bitcast(I32).rearrange("z (q r) c -> r q z c", r=4)
        for r in range(4):
            nc.sync.dma_start(x_scales[r:P:32, :, :].bitcast(I32), xs_rows[r])
        load_wb(1)
        for z in range(PASSES):
            nc.sync.dma_start(x_words[z][:], xt_words[z].rearrange("p t r -> p (t r)").bitcast(I32))
        for r in range(4):
            nc.sync.dma_start(a_scales[r:P:32, :, :].bitcast(I32), as_rows[r])
        nc.sync.dma_start(a_words[:], wa_words.rearrange("z p n r -> p z (n r)").bitcast(I32))

        for r in range(ROW_TILES):
            nc.vector.memset(pages[r][:], 0.0)
        make_identity(nc, ident[:])

        b_words = keep.tile([P, PASSES, N], U32, name="b_words", align_bytes=64)
        b_scales = keep.tile([P, PASSES, N], U8, name="b_scales", align_bytes=64)
        g_scales = keep.tile([P, PASSES, J], U8, name="g_scales", align_bytes=64)
        g_words = [keep.tile([P, J], U32, name=f"g_words{z}", align_bytes=64) for z in range(PASSES)]
        for z in range(PASSES):
            grouped = keep.tile([P, N, PACK], BF16, name=f"grouped{z}", align_bytes=64)
            nc.scalar.copy(
                grouped[:].rearrange("p (c i) t -> p c t i", i=4),
                wb_raw[z][:].rearrange("p t (c i) -> p c t i", i=4),
            )
            nc.vector.tensor_copy(g_scales[:, z, :], x_scales[:, z, :].indirect(tokens[:]))
            nc.vector.quantize_mx(
                out=b_words[:, z, :].bitcast(E4M3X4),
                scales=b_scales[:, z, :],
                in_=grouped[:].rearrange("p n t -> p (n t)"),
            )

        old_rows = []
        for r in range(ROW_TILES):
            tile = rows.tile([P, C], F32, name="rows")
            nc.sync.dma_start(tile[:], old[r * P : (r + 1) * P, :])
            old_rows.append(tile)

        bias_ps = psum.tile([P, N // P, P], F32, name="bias_ps")
        for c in range(N // P):
            nc.tensor.transpose(bias_ps[:, c, :], bias_cols[:, c : c + 1].to_broadcast([P, P]), ident[:])
        bias = keep.tile([P, N], F32, name="bias")
        nc.scalar.copy(bias[:].rearrange("m (p c) -> m p c", p=P), bias_ps[:].rearrange("m c p -> m p c"))

        nc.vector.tensor_copy(g_words[0][:], x_words[0][:].bitcast(U32).indirect(tokens[:]))
        for r in range(ROW_TILES):
            nc.vector.tensor_copy(
                g_words[1][:, r * P : (r + 1) * P],
                x_words[1][:].bitcast(U32).indirect(tokens[:, r * 8 : (r + 1) * 8]),
            )

        larger = []
        for r in range(ROW_TILES):
            slots = slice(r * P, (r + 1) * P)
            b_ps = psum.tile([P, N], F32, name=f"b_ps{r}")
            a_ps = psum.tile([P, N], F32, name=f"a_ps{r}")
            for acc, words, scales, fmt in ((b_ps, b_words, b_scales, E4M3X4), (a_ps, a_words, a_scales, E5M2X4)):
                for z in range(PASSES):
                    nc.tensor.matmul_mx(
                        out=acc[:],
                        lhsT=g_words[z][:, slots].bitcast(E5M2X4),
                        lhsT_scale=g_scales[:, z, slots],
                        rhs=words[:, z, :].bitcast(fmt),
                        rhs_scale=scales[:, z, :],
                        start=(z == 0),
                        stop=(z == PASSES - 1),
                    )
            biased = keep.tile([P, N], F32, name=f"biased{r}")
            nc.vector.tensor_tensor(biased[:], b_ps[:], bias[:], ALU.add)
            d = keep.tile([P, N], F32, name=f"larger{r}")
            nc.vector.tensor_tensor(d[:], a_ps[:], biased[:], ALU.max)
            larger.append(d)

        nc.scalar.activation(pages[0][:].indirect(places[:]), larger[0][:], COPY)
        nc.vector.tensor_copy(pages[1][:].indirect(places[:, 0:8]), larger[1][:, 0:P])
        nc.scalar.activation(pages[1][:].indirect(places[:, 8:16]), larger[1][:, P:N], COPY)

        for r in range(ROW_TILES):
            for c0 in range(0, C, STORE_COLS):
                cols = slice(c0, c0 + STORE_COLS)
                res = keep.tile([P, STORE_COLS], F32, name=f"res{r}_{c0}")
                nc.vector.scalar_tensor_tensor(
                    res[:], old_rows[r][:, cols], -0.4, pages[r][:, cols], ALU.mult, ALU.add
                )
                nc.sync.dma_start(out[r * P : (r + 1) * P, cols], res[:])
